import numpy as np
import ml_dtypes


def mxq(x, axis, fmt="e4m3"):
    dtype, down = {"e4m3": (ml_dtypes.float8_e4m3fn, 7), "e5m2": (ml_dtypes.float8_e5m2, 14)}[fmt]
    v = np.moveaxis(np.asarray(x, np.float32).astype(ml_dtypes.bfloat16).astype(np.float64), axis, -1)
    blocks = v.reshape(v.shape[:-1] + (-1, 32))
    amax = np.abs(blocks).max(-1, keepdims=True)
    byte = np.maximum(np.where(amax > 0, np.frexp(amax)[1] - 1 + 127, 0) - down, 1)
    scale = np.exp2(byte - 127.0)
    codes = (blocks / scale).astype(np.float32).astype(dtype).astype(np.float64)
    return np.moveaxis((codes * scale).reshape(v.shape), -1, axis)


WIDE = False


def mx_kscale(k):
    if not WIDE:
        return np.ones(k)
    levels = np.array([10, -10, 5, -5, 0])
    if k % 512:
        return np.exp2(np.random.permutation(np.resize(levels, k // 32))).repeat(32)
    a = np.empty((k // 512, 16))
    for p in range(k // 512):
        a[p, :8] = np.random.permutation(np.resize(levels, 8))
        for g in range(8):
            far = levels[np.abs(levels - a[p, g]) >= 10]
            a[p, g + 8] = far[np.random.randint(len(far))]
    return np.exp2(a.ravel()).repeat(32)


def f64(x):
    return np.asarray(x).astype(np.float64)


def striped(idx):
    return np.tile(np.asarray(idx).reshape(-1, 16).T, (8, 1)).astype(np.uint16)


def unstriped(offs):
    return offs[:16].T.reshape(-1).astype(np.int64)


def striped8(idx):
    return np.asarray(idx).reshape(8, -1, 16).transpose(0, 2, 1).reshape(128, -1).astype(np.uint16)


def unstriped8(offs):
    return offs.reshape(8, 16, -1).transpose(0, 2, 1).reshape(8, -1).astype(np.int64)


def pick8(x, idx, run):
    r = np.arange(len(x))
    return x[r[:, None], idx[r % (8 * run) // run]]


E2M1 = np.array([0.0, 0.5, 1.0, 1.5, 2.0, 3.0, 4.0, 6.0, -0.0, -0.5, -1.0, -1.5, -2.0, -3.0, -4.0, -6.0])


def pack_weight(w, fmt):
    k, n = w.shape
    w = f64(np.asarray(w, np.float32).astype(ml_dtypes.bfloat16)).reshape(k // 32, 32, n)
    amax = np.abs(w).max(1)
    if fmt == "e4m3":
        byte = np.frexp(amax)[1] - 1 + 127 - 7
    else:
        mant, ex = np.frexp(amax / 6.0)
        byte = np.where(mant > 0.5, ex, ex - 1) + 127
    byte = np.clip(np.where(amax > 0, byte, 1), 1, 254)
    scaled = (w * np.exp2(127.0 - byte)[:, None, :]).reshape(k, n).astype(np.float32)
    by_word = np.ascontiguousarray(scaled.reshape(k // 512, 128, 4, n).transpose(0, 1, 3, 2))
    if fmt == "e4m3":
        words = by_word.astype(ml_dtypes.float8_e4m3fn).view(np.uint8)
    else:
        c = by_word.astype(ml_dtypes.float4_e2m1fn).view(np.uint8) & 0xF
        words = (c[..., 0::2] | (c[..., 1::2] << 4)).reshape(k // 512, 128, 2 * n)
    return np.ascontiguousarray(words), np.ascontiguousarray(byte.astype(np.uint8).reshape(k // 512, 16, n))


def unpack_weight(words, scales, fmt):
    g, _, n = scales.shape
    words = np.ascontiguousarray(words).reshape(g, 128, n, -1)
    if fmt == "e4m3":
        vals = words.view(ml_dtypes.float8_e4m3fn).astype(np.float64)
    else:
        nib = np.empty((g, 128, n, 4), np.uint8)
        nib[..., 0::2] = words & 0xF
        nib[..., 1::2] = words >> 4
        vals = E2M1[nib]
    vals = vals * np.repeat(np.exp2(scales.astype(np.float64) - 127.0), 8, axis=1)[..., None]
    return vals.transpose(0, 1, 3, 2).reshape(g * 512, n)


K, J, R, T, Z, M, C, O, N, S, V, U, E = 512, 512, 512, 2048, 512, 1024, 1024, 256, 256, 512, 1024, 512, 1024


def setup_inputs():
    n = np.random.standard_normal
    idx = np.random.permutation(T)[:J]
    idx2 = np.random.permutation(M)[:J]
    idx3 = np.stack([np.random.permutation(C)[:J] for _ in range(8)])
    idx4 = np.stack([np.random.permutation(C)[:J] for _ in range(8)])
    idx5 = np.random.permutation(V)[:O]
    idx6 = np.stack([np.random.permutation(U)[:O] for _ in range(8)])
    idx7 = np.stack([np.random.permutation(E)[:U] for _ in range(8)])
    fk = mx_kscale(K)
    fr = mx_kscale(R)
    fz = mx_kscale(Z)
    fs = mx_kscale(S)
    xtp = pack_weight(n((K, T)) * fk[:, None], "e4m3")
    wp = pack_weight(n((K, R)) * 1 / np.sqrt(K) / fk[:, None] * fr, "e4m3")
    xop = pack_weight(n((Z, M)) / fz[:, None], "e4m3")
    w2p = pack_weight(n((Z, R)) * 1 / np.sqrt(Z) * fz[:, None] * fr, "e2m1")
    wbp = pack_weight(n((R, N)) * 1 / np.sqrt(R) / fr[:, None], "e2m1")
    xrp = pack_weight(n((S, V)) / fs[:, None], "e2m1")
    wsp = pack_weight(n((S, N)) * 1 / np.sqrt(S) * fs[:, None], "e4m3")
    return {
        "xt_words": xtp[0],
        "xt_scales": xtp[1],
        "w_words": wp[0],
        "w_scales": wp[1],
        "xo_words": xop[0],
        "xo_scales": xop[1],
        "w2_words": w2p[0],
        "w2_scales": w2p[1],
        "cf": (np.random.uniform(0.5, 1.6, (1, C))).astype(np.float32),
        "wb_words": wbp[0],
        "wb_scales": wbp[1],
        "xr_words": xrp[0],
        "xr_scales": xrp[1],
        "ws_words": wsp[0],
        "ws_scales": wsp[1],
        "tz": (np.random.randint(-7, 8, (N, E)).astype(np.float64)).astype(np.float32),
        "se": (np.random.randint(4, 15, (N, 1)) / 64.0).astype(np.float32),
        "offs": striped(idx),
        "offs2": striped(idx2),
        "offs3": striped8(idx3),
        "offs4": striped8(idx4),
        "offs5": striped(idx5),
        "offs6": striped8(idx6),
        "offs7": striped8(idx7),
    }


def reference(xt_words, xt_scales, w_words, w_scales, xo_words, xo_scales, w2_words, w2_scales, cf, wb_words, wb_scales, xr_words, xr_scales, ws_words, ws_scales, tz, se, offs, offs2, offs3, offs4, offs5, offs6, offs7):
    idx = unstriped(offs)
    idx2 = unstriped(offs2)
    idx3 = unstriped8(offs3)
    idx4 = unstriped8(offs4)
    idx5 = unstriped(offs5)
    idx6 = unstriped8(offs6)
    idx7 = unstriped8(offs7)
    xtu = unpack_weight(xt_words, xt_scales, "e4m3")
    wu = unpack_weight(w_words, w_scales, "e4m3")
    xou = unpack_weight(xo_words, xo_scales, "e4m3")
    w2u = unpack_weight(w2_words, w2_scales, "e2m1")
    wbu = unpack_weight(wb_words, wb_scales, "e2m1")
    xru = unpack_weight(xr_words, xr_scales, "e2m1")
    wsu = unpack_weight(ws_words, ws_scales, "e4m3")
    xtidxg = xtu[:, idx]
    a = wu.T @ xtidxg
    xoidx2g = xou[:, idx2]
    b = w2u.T @ xoidx2g
    pw = np.zeros((R, C))
    pw[np.arange(R)[:, None], idx3[np.arange(R) % 512 // 64]] = a
    pv = np.zeros((R, C))
    pv[np.arange(R)[:, None], idx4[np.arange(R) % 512 // 64]] = b
    g1 = np.maximum(pw, pv) * f64(cf)
    hid = g1.reshape(R, O, C // O).sum(axis=2)
    hidq = mxq(hid, 0, "e4m3")
    xridx5g = xru[:, idx5]
    p = wbu.T @ hidq + wsu.T @ xridx5g
    m0 = np.zeros((N, U))
    m0[np.arange(N)[:, None], idx6[np.arange(N) % 128 // 16]] = p
    y = np.maximum(m0, pick8(f64(tz), idx7, 16) * f64(se))
    return y

from contextlib import ExitStack

import concourse.mybir as mybir
from concourse.masks import make_identity

F32 = mybir.dt.float32
BF16 = mybir.dt.bfloat16
I32 = mybir.dt.int32
U32 = mybir.dt.uint32
U16 = mybir.dt.uint16
U8 = mybir.dt.uint8
FP8X4 = mybir.dt.float8_e4m3fn_x4
FP4X4 = mybir.dt.float4_e2m1fn_x4
COPY = mybir.ActivationFunctionType.Copy
MAX = mybir.AluOpType.max
MULT = mybir.AluOpType.mult
ADD = mybir.AluOpType.add
AXIS_X = mybir.AxisListType.X

P = 128
PACK = 4
J, R, T, M, C, O, N, V, U, E = 512, 512, 2048, 1024, 1024, 256, 256, 1024, 512, 1024
BUCKET = C // O
HALF_J = J // 2
HALF_O = O // 2
HALF_C = C // 2
LIST_ROWS = 16

FLOPS = 2 * 512 * (R * J + R * J + N * O + N * O)


def tile_picked_tokens_plain_two_wbuckets_reminder_endlevels_kernel(
    tc, xt_words, xt_scales, w_words, w_scales, xo_words, xo_scales, w2_words, w2_scales, cf,
    wb_words, wb_scales, xr_words, xr_scales, ws_words, ws_scales, tz, se,
    offs, offs2, offs3, offs4, offs5, offs6, offs7, out,
):
    nc = tc.nc
    with ExitStack() as ctx:
        keep = ctx.enter_context(tc.tile_pool(name="keep", bufs=1))
        ring = ctx.enter_context(tc.tile_pool(name="ring", bufs=2))
        psum = ctx.enter_context(tc.psum_pool(name="psum", bufs=1))
        psum_ab = ctx.enter_context(tc.psum_pool(name="psum_ab", bufs=4))

        def load_list(name, src):
            tile = keep.tile(list(src.shape), U16, name=name)
            nc.sync.dma_start(tile[:], src)
            return tile

        def load_fp8_words(name, src, tag=None):
            tile = keep.tile([P, src.shape[2]], I32, name=name, tag=tag or name, align_bytes=64)
            nc.sync.dma_start(tile[:], src[0].rearrange("p n t -> p (n t)").bitcast(I32))
            return tile

        def load_fp4_words(name, src, tag=None):
            tile = keep.tile([P, src.shape[2] // 2], U16, name=name, tag=tag or name, align_bytes=64)
            nc.sync.dma_start(tile[:].bitcast(I32), src[0].bitcast(I32))
            return tile

        def cleared_plane(name, src, tag=None, engine=nc.vector):
            tile = keep.tile([P, src.shape[2]], U8, name=name, tag=tag or name, align_bytes=64)
            engine.memset(tile[:].bitcast(I32), 0)
            return tile

        def load_scales(tile, src):
            for q in range(4):
                nc.sync.dma_start(tile[32 * q : 32 * q + 4, :].bitcast(I32), src[0, 4 * q : 4 * q + 4, :].bitcast(I32))

        def stage_scales(name, src):
            tile = keep.tile([4, 4, src.shape[2] // 4], I32, name=name, align_bytes=64)
            nc.sync.dma_start(tile[:], src[0].bitcast(I32).rearrange("(q r) n -> r q n", r=4))
            return tile

        def spread_scales(tile, staged):
            for q in range(4):
                nc.vector.tensor_copy(out=tile[32 * q : 32 * q + 4, :].bitcast(I32), in_=staged[:, q, :])

        def cleared_board(name, width, tag=None, engine=nc.vector):
            tile = keep.tile([P, width], F32, name=name, tag=tag or name, align_bytes=64)
            engine.memset(tile[:], 0.0)
            return tile

        def entries(lst, first, count):
            return lst[:, first // LIST_ROWS : (first + count) // LIST_ROWS]

        def dealt(view):
            return view.rearrange("p (t m) -> p m t", t=PACK)

        def natural(view):
            return view.rearrange("p (m t) -> p m t", t=PACK)

        xo_plane = cleared_plane("xo_plane", xo_scales, engine=nc.gpsimd)
        w2_plane_raw = cleared_plane("w2_plane_raw", w2_scales)
        xt_plane = cleared_plane("xt_plane", xt_scales)
        w_plane_raw = cleared_plane("w_plane_raw", w_scales)
        boards_b = [cleared_board("board_b0", C, engine=nc.gpsimd), cleared_board("board_b1", C)]

        l2 = load_list("l2", offs2)
        w2_staged = stage_scales("w2_staged", w2_scales)
        w2_raw = load_fp4_words("w2_raw", w2_words)
        l4 = load_list("l4", offs4)
        l1 = load_list("l1", offs)
        l3 = load_list("l3", offs3)
        l5 = load_list("l5", offs5)
        xo_table = load_fp8_words("xo_table", xo_words)
        load_scales(xo_plane, xo_scales)
        l6 = load_list("l6", offs6)
        l7 = load_list("l7", offs7)
        load_scales(xt_plane, xt_scales)
        load_scales(w_plane_raw, w_scales)

        spread_scales(w2_plane_raw, w2_staged)

        w2_codes = keep.tile([P, R], U16, name="w2_codes", align_bytes=64)
        w2_plane = keep.tile([P, R], U8, name="w2_plane", align_bytes=64)
        nc.scalar.copy(out=dealt(w2_codes[:]), in_=natural(w2_raw[:]))
        nc.vector.tensor_copy(out=dealt(w2_plane[:]), in_=natural(w2_plane_raw[:]))

        xt_table = load_fp8_words("xt_table", xt_words, tag="w2_raw")
        w_raw = load_fp8_words("w_raw", w_words, tag="w2_staged")

        xo_bytes = keep.tile([P, J], U8, name="xo_bytes", align_bytes=64)
        xo_codes = keep.tile([P, J], U32, name="xo_codes", align_bytes=64)
        for h in range(2):
            nc.vector.tensor_copy(
                out=xo_codes[:, h * HALF_J : (h + 1) * HALF_J],
                in_=xo_table[:].bitcast(U32).indirect(entries(l2, h * HALF_J, HALF_J)),
            )
            nc.vector.tensor_copy(
                out=xo_bytes[:, h * HALF_J : (h + 1) * HALF_J],
                in_=xo_plane[:].indirect(entries(l2, h * HALF_J, HALF_J)),
            )

        def product(lhs_codes, lhs_dtype, lhs_plane, rhs_codes, rhs_plane, t, cols):
            bank = psum_ab.tile([P, J], F32, name="bank")
            rows = slice(t * P, (t + 1) * P)
            nc.tensor.matmul_mx(
                out=bank[:, cols], lhsT=lhs_codes[:, rows].bitcast(lhs_dtype), lhsT_scale=lhs_plane[:, rows],
                rhs=rhs_codes[:, cols].bitcast(FP8X4), rhs_scale=rhs_plane[:, cols], start=True, stop=True,
            )
            return bank

        def scatter(board, lst, values, first, count):
            nc.scalar.activation(out=board[:].indirect(entries(lst, first, count)), in_=values, func=COPY)

        b_vals = [keep.tile([P, J], F32, name=f"b_vals{t}", align_bytes=64) for t in range(PACK)]
        for h in range(2):
            cols = slice(h * HALF_J, (h + 1) * HALF_J)
            bank = product(w2_codes, FP4X4, w2_plane, xo_codes, xo_bytes, 0, cols)
            if h == 0:
                nc.scalar.activation(out=b_vals[0][:, cols], in_=bank[:, cols], func=COPY)
            else:
                nc.vector.tensor_copy(out=b_vals[0][:, cols], in_=bank[:, cols])
            scatter(boards_b[0], l4, b_vals[0][:, cols], h * HALF_J, HALF_J)
        whole = slice(0, J)
        boards_b.append(cleared_board("board_b2", C, tag="xo_plane"))
        for t in range(1, 3):
            bank = product(w2_codes, FP4X4, w2_plane, xo_codes, xo_bytes, t, whole)
            nc.vector.tensor_copy(out=b_vals[t][:], in_=bank[:])
            scatter(boards_b[t], l4, b_vals[t][:], 0, J)

        boards_a = []
        w_codes = keep.tile([P, R], I32, name="w_codes", align_bytes=64)
        w_plane = keep.tile([P, R], U8, name="w_plane", align_bytes=64)
        xt_bytes = keep.tile([P, J], U8, name="xt_bytes", align_bytes=64)
        xt_codes = keep.tile([P, J], U32, name="xt_codes", align_bytes=64)
        nc.vector.tensor_copy(out=dealt(w_plane[:]), in_=natural(w_plane_raw[:]))
        nc.vector.tensor_copy(out=xt_bytes[:], in_=xt_plane[:].indirect(l1[:]))
        nc.vector.tensor_copy(out=dealt(w_codes[:]), in_=natural(w_raw[:]))
        nc.vector.tensor_copy(out=xt_codes[:], in_=xt_table[:].bitcast(U32).indirect(l1[:]))
        boards_a.append(cleared_board("board_a0", C, tag="w_plane_raw"))
        boards_a.append(cleared_board("board_a1", C, tag="xt_plane"))

        a_vals = [keep.tile([P, J], F32, name=f"a_vals{t}") for t in range(PACK - 1)]
        a_vals.append(keep.tile([P, J], F32, name="a_last", tag="late"))
        for t in range(PACK):
            bank = product(w_codes, FP8X4, w_plane, xt_codes, xt_bytes, t, whole)
            nc.vector.tensor_copy(out=a_vals[t][:], in_=bank[:])
        bank = product(w2_codes, FP4X4, w2_plane, xo_codes, xo_bytes, 3, whole)
        nc.vector.tensor_copy(out=b_vals[3][:], in_=bank[:])

        cf_rows = keep.tile([P, 2, BUCKET], F32, name="cf_rows", tag="w2_plane_raw", align_bytes=64)
        nc.sync.dma_start(cf_rows[:], cf[0].rearrange("(h p i) -> p h i", h=2, i=BUCKET))
        ident = keep.tile([P, P], F32, name="ident", tag="b_vals0", align_bytes=64)
        make_identity(nc, ident[:])
        weights = [psum.tile([P, BUCKET, HALF_O], F32, name=f"weights{h}") for h in range(2)]
        for h in range(2):
            for i in range(BUCKET):
                nc.tensor.transpose(weights[h][:, i, :], cf_rows[:, h, i : i + 1].to_broadcast([P, P]), ident[:])

        xr_plane = cleared_plane("xr_plane", xr_scales, tag="xo_bytes")
        ws_plane = cleared_plane("ws_plane", ws_scales, tag="w2_plane")
        wb_plane = cleared_plane("wb_plane", wb_scales, tag="w_plane")
        load_scales(xr_plane, xr_scales)
        load_scales(ws_plane, ws_scales)
        load_scales(wb_plane, wb_scales)
        xr_table = load_fp4_words("xr_table", xr_words, tag="w2_codes")
        ws_codes = load_fp8_words("ws_codes", ws_words, tag="w_codes")
        wb_codes = load_fp4_words("wb_codes", wb_words, tag="xt_bytes")
        pages = [cleared_board(f"page{u}", U, tag=tag) for u, tag in enumerate(("w2_staged", "w2_raw"))]
        xr_bytes = keep.tile([P, O], U8, name="xr_bytes", align_bytes=64)
        xr_codes = keep.tile([P, O], U16, name="xr_codes", align_bytes=64)
        nc.vector.tensor_copy(out=xr_bytes[:], in_=xr_plane[:].indirect(l5[:]))
        nc.vector.tensor_copy(out=xr_codes[:], in_=xr_table[:].indirect(l5[:]))
        steps = keep.tile([P, 2], F32, name="steps", tag="w2_plane_raw", align_bytes=64)
        nc.sync.dma_start(steps[:], se.rearrange("(u p) one -> p (u one)", p=P))
        levels = []
        for u, tag in enumerate(("xo_codes", "xt_codes")):
            levels.append(keep.tile([P, E], F32, name=f"levels{u}", tag=tag, align_bytes=64))
            nc.sync.dma_start(levels[u][:], tz[u * P : (u + 1) * P, :])
        sums = [psum.tile([P, 2, HALF_O], F32, name=f"sums{h}") for h in range(2)]
        for h in range(2):
            cols = slice(h * HALF_O, (h + 1) * HALF_O)
            for u in range(2):
                rows = slice(u * P, (u + 1) * P)
                nc.tensor.matmul_mx(
                    out=sums[h][:, u, :], lhsT=ws_codes[:, rows].bitcast(FP8X4), lhsT_scale=ws_plane[:, rows],
                    rhs=xr_codes[:, cols].bitcast(FP4X4), rhs_scale=xr_bytes[:, cols], start=(u == 0), stop=False,
                )

        hid = [keep.tile([P, HALF_O, PACK], BF16, name=f"hid{h}", align_bytes=64) for h in range(2)]

        def buckets(t, board_a, board_b, h, pieces):
            width = HALF_O // pieces
            larger = ring.tile([P, HALF_O, BUCKET], F32, name="larger")
            weighted = ring.tile([P, HALF_O, BUCKET], F32, name="weighted")
            spans = [slice(k * width, (k + 1) * width) for k in range(pieces)]
            side_a = board_a[:, h * HALF_C : (h + 1) * HALF_C].rearrange("p (o i) -> p o i", i=BUCKET)
            side_b = board_b[:, h * HALF_C : (h + 1) * HALF_C].rearrange("p (o i) -> p o i", i=BUCKET)
            for s in spans:
                nc.vector.tensor_tensor(out=larger[:, s, :], in0=side_a[:, s, :], in1=side_b[:, s, :], op=MAX)
            for s in spans:
                nc.vector.tensor_tensor(
                    out=weighted[:, s, :], in0=larger[:, s, :],
                    in1=weights[h][:].rearrange("p i o -> p o i")[:, s, :], op=MULT,
                )
            with nc.allow_low_precision(reason="the float32 bucket sum is rounded once, for the quantiser"):
                for s in spans:
                    nc.vector.tensor_reduce(out=hid[h][:, s, t], in_=weighted[:, s, :], axis=AXIS_X, op=ADD)

        for t in range(PACK - 1):
            scatter(boards_a[t % 2], l3, a_vals[t][:], 0, J)
            for h in range(2):
                buckets(t, boards_a[t % 2], boards_b[t], h, 1)
        scatter(boards_b[0], l4, b_vals[3][:], 0, J)
        scatter(boards_a[1], l3, a_vals[3][:], 0, J)

        leveled = keep.tile([P, 2, U], F32, name="leveled", tag="late")
        for u in range(2):
            nc.scalar.activation(
                out=leveled[:, u, :], in_=levels[u][:].indirect(l7[:]), func=COPY, scale=steps[:, u : u + 1]
            )

        for h in range(2):
            buckets(3, boards_a[1], boards_b[0], h, 2)
            hid_codes = keep.tile([P, HALF_O], U32, name=f"hid_codes{h}", align_bytes=64)
            hid_plane = keep.tile([P, HALF_O], U8, name=f"hid_plane{h}", align_bytes=64)
            nc.vector.quantize_mx(
                out=hid_codes[:].bitcast(FP8X4), scales=hid_plane[:], in_=hid[h][:].rearrange("p o t -> p (o t)")
            )
            for u in range(2):
                rows = slice(u * P, (u + 1) * P)
                nc.tensor.matmul_mx(
                    out=sums[h][:, u, :], lhsT=wb_codes[:, rows].bitcast(FP4X4), lhsT_scale=wb_plane[:, rows],
                    rhs=hid_codes[:].bitcast(FP8X4), rhs_scale=hid_plane[:], start=False, stop=(u == 1),
                )
            p_vals = keep.tile([P, 2, HALF_O], F32, name=f"p_vals{h}")
            if h == 0:
                nc.scalar.activation(out=p_vals[:], in_=sums[h][:], func=COPY)
            else:
                nc.vector.tensor_copy(out=p_vals[:], in_=sums[h][:])
            for u in range(2):
                scatter(pages[u], l6, p_vals[:, u, :], h * HALF_O, HALF_O)

        for u in range(2):
            result = keep.tile([P, U], F32, name=f"result{u}")
            nc.vector.tensor_tensor(out=result[:], in0=pages[u][:], in1=leveled[:, u, :], op=MAX)
            nc.sync.dma_start(out[u * P : (u + 1) * P, :], result[:])
